import numpy as np
import ml_dtypes


def mxq(x, axis, fmt="e4m3"):
    dtype, down = {"e4m3": (ml_dtypes.float8_e4m3fn, 7), "e5m2": (ml_dtypes.float8_e5m2, 14)}[fmt]
    v = np.moveaxis(np.asarray(x, np.float32).astype(ml_dtypes.bfloat16).astype(np.float64), axis, -1)
    blocks = v.reshape(v.shape[:-1] + (-1, 32))
    amax = np.abs(blocks).max(-1, keepdims=True)
    byte = np.maximum(np.where(amax > 0, np.frexp(amax)[1] - 1 + 127, 0) - down, 1)
    scale = np.exp2(byte - 127.0)
    codes = (blocks / scale).astype(np.float32).astype(dtype).astype(np.float64)
    return np.moveaxis((codes * scale).reshape(v.shape), -1, axis)


WIDE = False


def mx_kscale(k):
    if not WIDE:
        return np.ones(k)
    levels = np.array([10, -10, 5, -5, 0])
    if k % 512:
        return np.exp2(np.random.permutation(np.resize(levels, k // 32))).repeat(32)
    a = np.empty((k // 512, 16))
    for p in range(k // 512):
        a[p, :8] = np.random.permutation(np.resize(levels, 8))
        for g in range(8):
            far = levels[np.abs(levels - a[p, g]) >= 10]
            a[p, g + 8] = far[np.random.randint(len(far))]
    return np.exp2(a.ravel()).repeat(32)


def f64(x):
    return np.asarray(x).astype(np.float64)


def striped(idx):
    return np.tile(idx.reshape(-1, 16).T, (8, 1)).astype(np.uint16)


def unstriped(offs):
    return offs[:16].T.reshape(-1).astype(np.int64)


def striped8(idx):
    return np.concatenate([x.reshape(-1, 16).T for x in idx]).astype(np.uint16)


def runs(offs, k):
    lists = np.stack([offs[16 * r : 16 * r + 16].T.reshape(-1) for r in range(8)]).astype(np.int64)
    return lists[np.arange(k) % 512 // 64]


def pack_weight(w):
    k, n = w.shape
    w = f64(np.asarray(w, np.float32).astype(ml_dtypes.bfloat16)).reshape(k // 32, 32, n)
    amax = np.abs(w).max(1)
    byte = np.clip(np.where(amax > 0, np.frexp(amax)[1] - 1 + 127 - 7, 1), 1, 254)
    scaled = (w * np.exp2(127.0 - byte)[:, None, :]).reshape(k, n).astype(np.float32)
    words = np.ascontiguousarray(scaled.reshape(k // 512, 128, 4, n).transpose(0, 1, 3, 2)).astype(ml_dtypes.float8_e4m3fn).view(np.uint8)
    return words, np.ascontiguousarray(byte.astype(np.uint8).reshape(k // 512, 16, n))


def unpack_weight(words, scales):
    g, p, n, _ = words.shape
    vals = np.ascontiguousarray(words).view(ml_dtypes.float8_e4m3fn).astype(np.float64) * np.repeat(np.exp2(scales.astype(np.float64) - 127.0), 8, axis=1)[..., None]
    return vals.transpose(0, 1, 3, 2).reshape(g * 512, n)


def sigmoid(v):
    return 1.0 / (1.0 + np.exp(-np.maximum(v, -700.0)))


K, T, S, V, H = 512, 2048, 512, 512, 512


def setup_inputs():
    n = np.random.standard_normal
    s = mx_kscale(K)[:, None]
    u = mx_kscale(S)
    packed_xT = pack_weight(n((K, T)) * s)
    return {
        "x_words": packed_xT[0],
        "x_scales": packed_xT[1],
        "w1": (n((K, H)) / np.sqrt(K) / s).astype(np.float32),
        "w2": (n((K, H)) / np.sqrt(K) / s).astype(np.float32),
        "ga": (np.random.uniform(0.5, 1.5, (H, 1)) * u[:, None]).astype(np.float32),
        "gb": (np.random.uniform(0.5, 1.5, (H, 1)) / u[:, None]).astype(np.float32),
        "offs": striped(np.random.permutation(T)[:S]),
        "two": striped(np.random.permutation(T)[:V]),
        "n1": striped8(np.stack([np.random.permutation(S) for _ in range(8)])),
        "nq": striped8(np.stack([np.random.permutation(V) for _ in range(8)])),
        "cq": striped8(np.stack([np.random.permutation(V) for _ in range(8)])),
    }


def reference(x_words, x_scales, w1, w2, ga, gb, offs, two, n1, nq, cq):
    xq = unpack_weight(x_words, x_scales)[:, unstriped(offs)]
    a = mxq(f64(w1), 0, "e4m3").T @ xq
    z = f64(ga) * (a / (np.abs(a[np.arange(H)[:, None], runs(n1, H)]) + 0.5))
    x_two = unpack_weight(x_words, x_scales)[:, unstriped(two)]
    b = mxq(f64(w2), 0, "e4m3").T @ x_two
    z2 = f64(gb) * ((b[np.arange(H)[:, None], runs(nq, H)]) / (np.abs(b) + 0.5))
    s = 0.0625 * ((mxq(z, 0, "e4m3").T @ mxq(z2, 0, "e4m3")))
    return s * (sigmoid(s[np.arange(S)[:, None], runs(cq, S)]))

@@ -1,0 +1,193 @@
+from contextlib import ExitStack
+
+import concourse.mybir as mybir
+
+F32 = mybir.dt.float32
+BF16 = mybir.dt.bfloat16
+I32 = mybir.dt.int32
+U32 = mybir.dt.uint32
+U16 = mybir.dt.uint16
+U8 = mybir.dt.uint8
+FP8X4 = mybir.dt.float8_e4m3fn_x4
+ACT = mybir.ActivationFunctionType
+ALU = mybir.AluOpType
+
+P = 128
+PACK = 4
+T = 2048
+N = 512
+HALF = N // 2
+LIST_COLS = N // 16
+M_ON_SCALAR = 40
+
+FLOPS = 3 * 2 * 512 * 512 * 512
+
+
+def tile_picked_keynorm_none_p_kernel(tc, x_words, x_scales, w1, w2, ga, gb, offs, two, n1, nq, cq, out):
+    nc = tc.nc
+    halves = [(slice(h * HALF, (h + 1) * HALF), slice(h * LIST_COLS // 2, (h + 1) * LIST_COLS // 2)) for h in range(2)]
+
+    with ExitStack() as ctx:
+        lists = ctx.enter_context(tc.tile_pool(name="lists", bufs=1))
+        keep = ctx.enter_context(tc.tile_pool(name="keep", bufs=1))
+        psum = ctx.enter_context(tc.psum_pool(name="psum", bufs=1))
+
+        offs_sb = lists.tile([P, LIST_COLS], U16, name="offs_sb")
+        two_sb = lists.tile([P, LIST_COLS], U16, name="two_sb")
+        n1_sb = lists.tile([P, LIST_COLS], U16, name="n1_sb")
+        nq_sb = lists.tile([P, LIST_COLS], U16, name="nq_sb")
+        cq_sb = lists.tile([P, LIST_COLS], U16, name="cq_sb")
+
+        xw = keep.tile([P, T], U32, name="xw", align_bytes=64)
+        xs = keep.tile([P, T], U8, name="xs", align_bytes=64)
+        ga_sb = keep.tile([P, PACK], F32, name="ga_sb")
+        gb_sb = keep.tile([P, PACK], F32, name="gb_sb")
+
+        nc.vector.memset(xs[:].bitcast(I32), 0)
+        one = keep.tile([P, 1], F32, name="one", tag="w2_raw")
+        nc.vector.memset(one[:], 1.0)
+        warm_ln = keep.tile([P, 1], F32, name="warm_ln", tag="w1_raw")
+        nc.scalar.activation(warm_ln[:], one[:], ACT.Ln)
+
+        w2_raw = keep.tile([P, PACK, N], F32, name="w2_raw", tag="w2_raw")
+        w1_raw = keep.tile([P, PACK, N], F32, name="w1_raw", tag="w1_raw")
+
+        nc.sync.dma_start(two_sb[:], two)
+        nc.sync.dma_start(offs_sb[:], offs)
+        nc.sync.dma_start(nq_sb[:], nq)
+        nc.sync.dma_start(xw[:].bitcast(I32), x_words[0].rearrange("p n r -> p (n r)").bitcast(I32))
+        nc.sync.dma_start(n1_sb[:], n1)
+        nc.sync.dma_start(cq_sb[:], cq)
+        for q in range(4):
+            nc.sync.dma_start(xs[32 * q : 32 * q + 4, :].bitcast(I32), x_scales[0, 4 * q : 4 * q + 4, :].bitcast(I32))
+        nc.sync.dma_start(w2_raw[:], w2.rearrange("(p j) c -> p j c", j=PACK))
+        nc.sync.dma_start(w1_raw[:], w1.rearrange("(p j) c -> p j c", j=PACK))
+        nc.gpsimd.dma_start(gb_sb[:], gb.rearrange("(p t) o -> p (t o)", t=PACK))
+        nc.gpsimd.dma_start(ga_sb[:], ga.rearrange("(p t) o -> p (t o)", t=PACK))
+
+        def mx_tiles(name):
+            codes = keep.tile([P, N], U32, name=name + "_codes", align_bytes=64)
+            scales = keep.tile([P, N], U8, name=name + "_scales", align_bytes=64)
+            return codes, scales
+
+        def quantize(dst, grouped, first, count):
+            codes, scales = dst
+            nc.vector.quantize_mx(
+                out=codes[:, first : first + count].bitcast(FP8X4),
+                scales=scales[:, first : first + count],
+                in_=grouped[:, PACK * first : PACK * (first + count)],
+            )
+
+        def product(bank, stationary, t, moving):
+            cols = slice(t * P, (t + 1) * P)
+            nc.tensor.matmul_mx(
+                out=bank[:],
+                lhsT=stationary[0][:, cols].bitcast(FP8X4),
+                lhsT_scale=stationary[1][:, cols],
+                rhs=moving[0][:].bitcast(FP8X4),
+                rhs_scale=moving[1][:],
+                start=True,
+                stop=True,
+            )
+
+        def dealt_views(grouped, planes):
+            return (
+                grouped[:].rearrange("p (t m j) -> p m j t", t=PACK, j=PACK),
+                planes[:].rearrange("p j (m t) -> p m j t", t=PACK),
+            )
+
+        x_two = mx_tiles("x_two")
+        x_idx_scales = keep.tile([P, N], U8, name="x_idx_scales", align_bytes=64)
+        nc.vector.tensor_copy(x_two[1][:], xs[:].indirect(two_sb[:]))
+        nc.vector.tensor_copy(x_two[0][:], xw[:].indirect(two_sb[:]))
+        nc.vector.tensor_copy(x_idx_scales[:], xs[:].indirect(offs_sb[:]))
+
+        w2_grouped = keep.tile([P, PACK * N], BF16, name="w2_grouped", tag="w2_grouped", align_bytes=64)
+        dst, src = dealt_views(w2_grouped, w2_raw)
+        nc.scalar.copy(dst[:, :M_ON_SCALAR], src[:, :M_ON_SCALAR])
+        nc.vector.tensor_copy(dst[:, M_ON_SCALAR:], src[:, M_ON_SCALAR:])
+        w2_mx = mx_tiles("w2")
+        b_banks = [psum.tile([P, N], F32, name="b_bank%d" % t, tag="bank%d" % t) for t in range(PACK)]
+        for t in range(PACK):
+            quantize(w2_mx, w2_grouped, t * P, P)
+            product(b_banks[t], w2_mx, t, x_two)
+
+        x_idx_codes = keep.tile([P, N], U32, name="x_idx_codes", tag="w2_grouped", align_bytes=64)
+        nc.vector.tensor_copy(x_idx_codes[:], xw[:].indirect(offs_sb[:]))
+        x_idx = (x_idx_codes, x_idx_scales)
+
+        abs_b = keep.tile([P, PACK, N], F32, name="abs_b")
+        b_rows = [keep.tile([P, N], F32, name="b_row%d" % t) for t in range(PACK)]
+        for t in range(PACK):
+            nc.scalar.activation(abs_b[:, t, :], b_banks[t][:], ACT.Abs)
+            nc.vector.tensor_scalar_mul(b_rows[t][:], b_banks[t][:], gb_sb[:, t : t + 1])
+        log_b = keep.tile([P, PACK, N], F32, name="log_b", tag="log_b")
+        nc.scalar.activation(log_b[:], abs_b[:], ACT.Ln, bias=0.5)
+
+        w1_grouped = keep.tile([P, PACK * N], BF16, name="w1_grouped", tag="w1_grouped", align_bytes=64)
+        dst, src = dealt_views(w1_grouped, w1_raw)
+        nc.vector.tensor_copy(dst, src)
+        w1_mx = mx_tiles("w1")
+        a_banks = [psum.tile([P, N], F32, name="a_bank%d" % t, tag="bank%d" % (PACK + t)) for t in range(PACK)]
+        quantize(w1_mx, w1_grouped, 0, N)
+        for t in range(PACK):
+            product(a_banks[t], w1_mx, t, x_idx)
+
+        b_picked = keep.tile([P, PACK, N], F32, name="b_picked", tag="w1_grouped", align_bytes=64)
+        for t in range(PACK):
+            for cols, entries in halves:
+                nc.vector.tensor_copy(b_picked[:, t, cols], b_rows[t][:].indirect(nq_sb[:, entries]))
+
+        abs_a = keep.tile([P, PACK, N], F32, name="abs_a", tag="abs_a")
+        log_a = [keep.tile([P, N], F32, name="log_a%d" % t) for t in range(PACK)]
+        for t in range(PACK):
+            nc.scalar.activation(abs_a[:, t, :], a_banks[t][:], ACT.Abs)
+            nc.scalar.activation(log_a[t][:], abs_a[:, t, :], ACT.Ln, bias=0.5)
+
+        inv_b = keep.tile([P, PACK, N], F32, name="inv_b", tag="abs_a")
+        z2_grouped = keep.tile([P, PACK * N], BF16, name="z2_grouped", align_bytes=64)
+        z2_mx = mx_tiles("z2")
+        for h in range(2):
+            cols = halves[h][0]
+            nc.scalar.activation(inv_b[:, :, cols], log_b[:, :, cols], ACT.Exp, scale=-1.0)
+            nc.vector.tensor_tensor(
+                z2_grouped[:, PACK * h * HALF : PACK * (h + 1) * HALF].rearrange("p (c i t) -> p c t i", i=4, t=PACK),
+                b_picked[:, :, cols].rearrange("p t (c i) -> p c t i", i=4),
+                inv_b[:, :, cols].rearrange("p t (c i) -> p c t i", i=4),
+                ALU.mult,
+            )
+            quantize(z2_mx, z2_grouped, h * HALF, HALF)
+
+        inv_a = keep.tile([P, PACK, N], F32, name="inv_a", tag="log_b")
+        z_planes = keep.tile([P, PACK, N], BF16, name="z_planes")
+        z_grouped = keep.tile([P, PACK * N], BF16, name="z_grouped", align_bytes=64)
+        dst, src = dealt_views(z_grouped, z_planes)
+        for h in range(2):
+            cols, entries = halves[h]
+            for t in range(PACK):
+                nc.scalar.activation(inv_a[:, t, cols], log_a[t][:].indirect(n1_sb[:, entries]), ACT.Exp, scale=-1.0)
+                nc.vector.scalar_tensor_tensor(
+                    z_planes[:, t, cols], a_banks[t][:, cols], ga_sb[:, t : t + 1], inv_a[:, t, cols], ALU.mult, ALU.mult
+                )
+            ms = slice(h * P // 2, (h + 1) * P // 2)
+            nc.vector.tensor_copy(dst[:, ms], src[:, ms])
+        warm_sigmoid = keep.tile([P, 1], F32, name="warm_sigmoid")
+        nc.scalar.activation(warm_sigmoid[:], inv_a[:, PACK - 1, N - 1 : N], ACT.Sigmoid)
+
+        z_mx = mx_tiles("z")
+        out_rows = out.rearrange("(p t) v -> p t v", t=PACK)
+        s_banks = [psum.tile([P, N], F32, name="s_bank%d" % t, tag="bank%d" % t) for t in range(PACK)]
+        for t in range(PACK):
+            quantize(z_mx, z_grouped, t * P, P)
+            product(s_banks[t], z_mx, t, z2_mx)
+        s_rows = [keep.tile([P, N], F32, name="s_row%d" % t) for t in range(PACK)]
+        gate = keep.tile([P, PACK, N], F32, name="gate")
+        result = keep.tile([P, PACK, N], F32, name="result")
+        for t in range(PACK):
+            nc.vector.tensor_scalar_mul(s_rows[t][:], s_banks[t][:], 0.0625)
+            for cols, entries in halves:
+                nc.scalar.activation(gate[:, t, cols], s_rows[t][:].indirect(cq_sb[:, entries]), ACT.Sigmoid)
+        for t in range(PACK):
+            for cols, entries in halves:
+                nc.vector.tensor_tensor(result[:, t, cols], s_rows[t][:, cols], gate[:, t, cols], ALU.mult)
+            nc.sync.dma_start(out_rows[:, t, :], result[:, t, :])

@@ -18,7 +18,7 @@ T = 2048
 N = 512
 HALF = N // 2
 LIST_COLS = N // 16
-M_ON_SCALAR = 40
+M_ON_SCALAR = 44
 
 FLOPS = 3 * 2 * 512 * 512 * 512
 
@@ -30,6 +30,8 @@ def tile_picked_keynorm_none_p_kernel(tc, x_words, x_scales, w1, w2, ga, gb, off
     with ExitStack() as ctx:
         lists = ctx.enter_context(tc.tile_pool(name="lists", bufs=1))
         keep = ctx.enter_context(tc.tile_pool(name="keep", bufs=1))
+        w2_bytes = ctx.enter_context(tc.tile_pool(name="w2_bytes", bufs=1))
+        w1_bytes = ctx.enter_context(tc.tile_pool(name="w1_bytes", bufs=1))
         psum = ctx.enter_context(tc.psum_pool(name="psum", bufs=1))
 
         offs_sb = lists.tile([P, LIST_COLS], U16, name="offs_sb")
@@ -38,29 +40,29 @@ def tile_picked_keynorm_none_p_kernel(tc, x_words, x_scales, w1, w2, ga, gb, off
         nq_sb = lists.tile([P, LIST_COLS], U16, name="nq_sb")
         cq_sb = lists.tile([P, LIST_COLS], U16, name="cq_sb")
 
-        xw = keep.tile([P, T], U32, name="xw", align_bytes=64)
         xs = keep.tile([P, T], U8, name="xs", align_bytes=64)
         ga_sb = keep.tile([P, PACK], F32, name="ga_sb")
         gb_sb = keep.tile([P, PACK], F32, name="gb_sb")
 
         nc.vector.memset(xs[:].bitcast(I32), 0)
-        one = keep.tile([P, 1], F32, name="one", tag="w2_raw")
+        one = keep.tile([P, 1], F32, name="one", tag="xw", align_bytes=64)
         nc.vector.memset(one[:], 1.0)
-        warm_ln = keep.tile([P, 1], F32, name="warm_ln", tag="w1_raw")
+        warm_ln = w1_bytes.tile([P, 1], F32, name="warm_ln", offset=0)
         nc.scalar.activation(warm_ln[:], one[:], ACT.Ln)
 
-        w2_raw = keep.tile([P, PACK, N], F32, name="w2_raw", tag="w2_raw")
-        w1_raw = keep.tile([P, PACK, N], F32, name="w1_raw", tag="w1_raw")
+        xw = keep.tile([P, T], U32, name="xw", tag="xw", align_bytes=64)
+        w2_raw = keep.tile([P, PACK, N], F32, name="w2_raw")
+        w1_raw = w1_bytes.tile([P, PACK, N], F32, name="w1_raw", offset=0)
 
         nc.sync.dma_start(two_sb[:], two)
         nc.sync.dma_start(offs_sb[:], offs)
         nc.sync.dma_start(nq_sb[:], nq)
-        nc.sync.dma_start(xw[:].bitcast(I32), x_words[0].rearrange("p n r -> p (n r)").bitcast(I32))
+        nc.sync.dma_start(w2_raw[:], w2.rearrange("(p j) c -> p j c", j=PACK))
         nc.sync.dma_start(n1_sb[:], n1)
         nc.sync.dma_start(cq_sb[:], cq)
         for q in range(4):
             nc.sync.dma_start(xs[32 * q : 32 * q + 4, :].bitcast(I32), x_scales[0, 4 * q : 4 * q + 4, :].bitcast(I32))
-        nc.sync.dma_start(w2_raw[:], w2.rearrange("(p j) c -> p j c", j=PACK))
+        nc.sync.dma_start(xw[:].bitcast(I32), x_words[0].rearrange("p n r -> p (n r)").bitcast(I32))
         nc.sync.dma_start(w1_raw[:], w1.rearrange("(p j) c -> p j c", j=PACK))
         nc.gpsimd.dma_start(gb_sb[:], gb.rearrange("(p t) o -> p (t o)", t=PACK))
         nc.gpsimd.dma_start(ga_sb[:], ga.rearrange("(p t) o -> p (t o)", t=PACK))
@@ -68,7 +70,7 @@ def tile_picked_keynorm_none_p_kernel(tc, x_words, x_scales, w1, w2, ga, gb, off
         def mx_tiles(name):
             codes = keep.tile([P, N], U32, name=name + "_codes", align_bytes=64)
             scales = keep.tile([P, N], U8, name=name + "_scales", align_bytes=64)
-            return codes, scales
+            return codes[:], scales[:]
 
         def quantize(dst, grouped, first, count):
             codes, scales = dst
@@ -84,8 +86,8 @@ def tile_picked_keynorm_none_p_kernel(tc, x_words, x_scales, w1, w2, ga, gb, off
                 out=bank[:],
                 lhsT=stationary[0][:, cols].bitcast(FP8X4),
                 lhsT_scale=stationary[1][:, cols],
-                rhs=moving[0][:].bitcast(FP8X4),
-                rhs_scale=moving[1][:],
+                rhs=moving[0].bitcast(FP8X4),
+                rhs_scale=moving[1],
                 start=True,
                 stop=True,
             )
@@ -96,33 +98,25 @@ def tile_picked_keynorm_none_p_kernel(tc, x_words, x_scales, w1, w2, ga, gb, off
                 planes[:].rearrange("p j (m t) -> p m j t", t=PACK),
             )
 
-        x_two = mx_tiles("x_two")
-        x_idx_scales = keep.tile([P, N], U8, name="x_idx_scales", align_bytes=64)
-        nc.vector.tensor_copy(x_two[1][:], xs[:].indirect(two_sb[:]))
-        nc.vector.tensor_copy(x_two[0][:], xw[:].indirect(two_sb[:]))
-        nc.vector.tensor_copy(x_idx_scales[:], xs[:].indirect(offs_sb[:]))
-
-        w2_grouped = keep.tile([P, PACK * N], BF16, name="w2_grouped", tag="w2_grouped", align_bytes=64)
+        w2_grouped = w2_bytes.tile([P, PACK * N], BF16, name="w2_grouped", offset=0, align_bytes=64)
         dst, src = dealt_views(w2_grouped, w2_raw)
         nc.scalar.copy(dst[:, :M_ON_SCALAR], src[:, :M_ON_SCALAR])
         nc.vector.tensor_copy(dst[:, M_ON_SCALAR:], src[:, M_ON_SCALAR:])
+        x_two_scales = keep.tile([P, N], U8, name="x_two_scales", align_bytes=64)
+        nc.vector.tensor_copy(x_two_scales[:], xs[:].indirect(two_sb[:]))
         w2_mx = mx_tiles("w2")
+        quantize(w2_mx, w2_grouped, 0, N)
+        x_two_codes = w2_bytes.tile([P, N], U32, name="x_two_codes", offset=0, align_bytes=64)
+        x_idx_codes = w2_bytes.tile([P, N], U32, name="x_idx_codes", offset=4 * N, align_bytes=64)
+        nc.vector.tensor_copy(x_two_codes[:], xw[:].indirect(two_sb[:]))
+        nc.vector.tensor_copy(x_idx_codes[:], xw[:].indirect(offs_sb[:]))
+        x_idx_scales = keep.tile([P, N], U8, name="x_idx_scales", tag="xw", align_bytes=64)
+        nc.vector.tensor_copy(x_idx_scales[:], xs[:].indirect(offs_sb[:]))
+        x_two = (x_two_codes[:], x_two_scales[:])
+        x_idx = (x_idx_codes[:], x_idx_scales[:])
         b_banks = [psum.tile([P, N], F32, name="b_bank%d" % t, tag="bank%d" % t) for t in range(PACK)]
         for t in range(PACK):
-            quantize(w2_mx, w2_grouped, t * P, P)
             product(b_banks[t], w2_mx, t, x_two)
-
-        x_idx_codes = keep.tile([P, N], U32, name="x_idx_codes", tag="w2_grouped", align_bytes=64)
-        nc.vector.tensor_copy(x_idx_codes[:], xw[:].indirect(offs_sb[:]))
-        x_idx = (x_idx_codes, x_idx_scales)
-
-        abs_b = keep.tile([P, PACK, N], F32, name="abs_b")
-        b_rows = [keep.tile([P, N], F32, name="b_row%d" % t) for t in range(PACK)]
-        for t in range(PACK):
-            nc.scalar.activation(abs_b[:, t, :], b_banks[t][:], ACT.Abs)
-            nc.vector.tensor_scalar_mul(b_rows[t][:], b_banks[t][:], gb_sb[:, t : t + 1])
-        log_b = keep.tile([P, PACK, N], F32, name="log_b", tag="log_b")
-        nc.scalar.activation(log_b[:], abs_b[:], ACT.Ln, bias=0.5)
 
         w1_grouped = keep.tile([P, PACK * N], BF16, name="w1_grouped", tag="w1_grouped", align_bytes=64)
         dst, src = dealt_views(w1_grouped, w1_raw)
@@ -132,6 +126,14 @@ def tile_picked_keynorm_none_p_kernel(tc, x_words, x_scales, w1, w2, ga, gb, off
         quantize(w1_mx, w1_grouped, 0, N)
         for t in range(PACK):
             product(a_banks[t], w1_mx, t, x_idx)
+
+        abs_b = keep.tile([P, PACK, N], F32, name="abs_b")
+        b_rows = [w1_bytes.tile([P, N], F32, name="b_row%d" % t, offset=4 * N * t) for t in range(PACK)]
+        for t in range(PACK):
+            nc.scalar.activation(abs_b[:, t, :], b_banks[t][:], ACT.Abs)
+            nc.vector.tensor_scalar_mul(b_rows[t][:], b_banks[t][:], gb_sb[:, t : t + 1])
+        log_b = keep.tile([P, PACK, N], F32, name="log_b", tag="log_b")
+        nc.scalar.activation(log_b[:], abs_b[:], ACT.Ln, bias=0.5)
 
         b_picked = keep.tile([P, PACK, N], F32, name="b_picked", tag="w1_grouped", align_bytes=64)
         for t in range(PACK):
@@ -170,24 +172,52 @@ def tile_picked_keynorm_none_p_kernel(tc, x_words, x_scales, w1, w2, ga, gb, off
                     z_planes[:, t, cols], a_banks[t][:, cols], ga_sb[:, t : t + 1], inv_a[:, t, cols], ALU.mult, ALU.mult
                 )
             ms = slice(h * P // 2, (h + 1) * P // 2)
-            nc.vector.tensor_copy(dst[:, ms], src[:, ms])
+            if h == 0:
+                nc.vector.tensor_copy(dst[:, ms], src[:, ms])
+            else:
+                nc.vector.tensor_copy(dst[:, ms, :, :1], src[:, ms, :, :1])
         warm_sigmoid = keep.tile([P, 1], F32, name="warm_sigmoid")
         nc.scalar.activation(warm_sigmoid[:], inv_a[:, PACK - 1, N - 1 : N], ACT.Sigmoid)
 
         z_mx = mx_tiles("z")
         out_rows = out.rearrange("(p t) v -> p t v", t=PACK)
-        s_banks = [psum.tile([P, N], F32, name="s_bank%d" % t, tag="bank%d" % t) for t in range(PACK)]
-        for t in range(PACK):
-            quantize(z_mx, z_grouped, t * P, P)
-            product(s_banks[t], z_mx, t, z2_mx)
-        s_rows = [keep.tile([P, N], F32, name="s_row%d" % t) for t in range(PACK)]
+        last = PACK - 1
+        first_banks = [psum.tile([P, HALF], F32, name="first_bank%d" % h, tag="bank%d" % (PACK * h)) for h in range(2)]
+        s_banks = [None] + [psum.tile([P, N], F32, name="s_bank%d" % t, tag="bank%d" % t) for t in range(1, PACK)]
+        rows = [keep.tile([P, N], F32, name="row%d" % t) for t in range(PACK)]
         gate = keep.tile([P, PACK, N], F32, name="gate")
         result = keep.tile([P, PACK, N], F32, name="result")
-        for t in range(PACK):
-            nc.vector.tensor_scalar_mul(s_rows[t][:], s_banks[t][:], 0.0625)
+
+        quantize(z_mx, z_grouped, 0, P)
+        for h in range(2):
+            cols = halves[h][0]
+            product(first_banks[h], z_mx, 0, (z2_mx[0][:, cols], z2_mx[1][:, cols]))
+        nc.vector.tensor_copy(dst[:, P // 2 :, :, 1:], src[:, P // 2 :, :, 1:])
+        for t in range(1, PACK):
+            quantize(z_mx, z_grouped, t * P, P)
+            product(s_banks[t], z_mx, t, z2_mx)
+        for h in range(2):
+            nc.vector.tensor_scalar_mul(rows[0][:, halves[h][0]], first_banks[h][:], 0.0625)
+        for t in range(1, last):
+            nc.vector.tensor_scalar_mul(rows[t][:], s_banks[t][:], 0.0625)
+
+        def gate_on_scalar(t):
             for cols, entries in halves:
-                nc.scalar.activation(gate[:, t, cols], s_rows[t][:].indirect(cq_sb[:, entries]), ACT.Sigmoid)
-        for t in range(PACK):
-            for cols, entries in halves:
-                nc.vector.tensor_tensor(result[:, t, cols], s_rows[t][:, cols], gate[:, t, cols], ALU.mult)
-            nc.sync.dma_start(out_rows[:, t, :], result[:, t, :])
+                nc.scalar.activation(gate[:, t, cols], rows[t][:].indirect(cq_sb[:, entries]), ACT.Sigmoid)
+
+        def finish(t, pieces):
+            for cols in pieces:
+                nc.vector.tensor_tensor(result[:, t, cols], rows[t][:, cols], gate[:, t, cols], ALU.mult)
+                nc.sync.dma_start(out_rows[:, t, cols], result[:, t, cols])
+
+        gate_on_scalar(0)
+        nc.scalar.activation(rows[last][:], s_banks[last][:], ACT.Sigmoid, scale=0.0625)
+        gate_on_scalar(1)
+        gate_on_scalar(2)
+        finish(0, [slice(0, N)])
+        for cols, entries in halves:
+            nc.vector.tensor_copy(gate[:, last, cols], rows[last][:].indirect(cq_sb[:, entries]))
+        nc.vector.scalar_tensor_tensor(result[:, last, :], s_banks[last][:], 0.0625, gate[:, last, :], ALU.mult, ALU.mult)
+        nc.sync.dma_start(out_rows[:, last, :], result[:, last, :])
+        finish(1, [slice(0, N)])
+        finish(2, [cols for cols, entries in halves])

@@ -18,7 +18,9 @@ T = 2048
 N = 512
 HALF = N // 2
 LIST_COLS = N // 16
-M_ON_SCALAR = 44
+M_ON_SCALAR = 40
+
+SMALLEST_NORMAL = 2.0**-126
 
 FLOPS = 3 * 2 * 512 * 512 * 512
 
@@ -30,7 +32,6 @@ def tile_picked_keynorm_none_p_kernel(tc, x_words, x_scales, w1, w2, ga, gb, off
     with ExitStack() as ctx:
         lists = ctx.enter_context(tc.tile_pool(name="lists", bufs=1))
         keep = ctx.enter_context(tc.tile_pool(name="keep", bufs=1))
-        w2_bytes = ctx.enter_context(tc.tile_pool(name="w2_bytes", bufs=1))
         w1_bytes = ctx.enter_context(tc.tile_pool(name="w1_bytes", bufs=1))
         psum = ctx.enter_context(tc.psum_pool(name="psum", bufs=1))
 
@@ -45,24 +46,27 @@ def tile_picked_keynorm_none_p_kernel(tc, x_words, x_scales, w1, w2, ga, gb, off
         gb_sb = keep.tile([P, PACK], F32, name="gb_sb")
 
         nc.vector.memset(xs[:].bitcast(I32), 0)
-        one = keep.tile([P, 1], F32, name="one", tag="xw", align_bytes=64)
+        one = keep.tile([P, 16], F32, name="one", tag="w2_left")
         nc.vector.memset(one[:], 1.0)
-        warm_ln = w1_bytes.tile([P, 1], F32, name="warm_ln", offset=0)
+        warm_ln = w1_bytes.tile([P, 16], F32, name="warm_ln", offset=16 * N - 32)
         nc.scalar.activation(warm_ln[:], one[:], ACT.Ln)
 
-        xw = keep.tile([P, T], U32, name="xw", tag="xw", align_bytes=64)
-        w2_raw = keep.tile([P, PACK, N], F32, name="w2_raw")
+        xw = keep.tile([P, T], U32, name="xw", align_bytes=64)
+        w2_left = keep.tile([P, PACK, HALF], F32, name="w2_left", tag="w2_left")
+        w2_right = w1_bytes.tile([P, PACK, HALF], F32, name="w2_right", offset=16 * N)
         w1_raw = w1_bytes.tile([P, PACK, N], F32, name="w1_raw", offset=0)
 
         nc.sync.dma_start(two_sb[:], two)
         nc.sync.dma_start(offs_sb[:], offs)
         nc.sync.dma_start(nq_sb[:], nq)
-        nc.sync.dma_start(w2_raw[:], w2.rearrange("(p j) c -> p j c", j=PACK))
+        nc.sync.dma_start(xw[:].bitcast(I32), x_words[0].rearrange("p n r -> p (n r)").bitcast(I32))
         nc.sync.dma_start(n1_sb[:], n1)
         nc.sync.dma_start(cq_sb[:], cq)
         for q in range(4):
             nc.sync.dma_start(xs[32 * q : 32 * q + 4, :].bitcast(I32), x_scales[0, 4 * q : 4 * q + 4, :].bitcast(I32))
-        nc.sync.dma_start(xw[:].bitcast(I32), x_words[0].rearrange("p n r -> p (n r)").bitcast(I32))
+        w2_rows = w2.rearrange("(p j) c -> p j c", j=PACK)
+        nc.sync.dma_start(w2_left[:], w2_rows[:, :, :HALF])
+        nc.sync.dma_start(w2_right[:], w2_rows[:, :, HALF:])
         nc.sync.dma_start(w1_raw[:], w1.rearrange("(p j) c -> p j c", j=PACK))
         nc.gpsimd.dma_start(gb_sb[:], gb.rearrange("(p t) o -> p (t o)", t=PACK))
         nc.gpsimd.dma_start(ga_sb[:], ga.rearrange("(p t) o -> p (t o)", t=PACK))
@@ -98,25 +102,27 @@ def tile_picked_keynorm_none_p_kernel(tc, x_words, x_scales, w1, w2, ga, gb, off
                 planes[:].rearrange("p j (m t) -> p m j t", t=PACK),
             )
 
-        w2_grouped = w2_bytes.tile([P, PACK * N], BF16, name="w2_grouped", offset=0, align_bytes=64)
-        dst, src = dealt_views(w2_grouped, w2_raw)
-        nc.scalar.copy(dst[:, :M_ON_SCALAR], src[:, :M_ON_SCALAR])
-        nc.vector.tensor_copy(dst[:, M_ON_SCALAR:], src[:, M_ON_SCALAR:])
+        x_two_codes = keep.tile([P, N], U32, name="x_two_codes", align_bytes=64)
+        x_idx_codes = keep.tile([P, N], U32, name="x_idx_codes", align_bytes=64)
         x_two_scales = keep.tile([P, N], U8, name="x_two_scales", align_bytes=64)
-        nc.vector.tensor_copy(x_two_scales[:], xs[:].indirect(two_sb[:]))
-        w2_mx = mx_tiles("w2")
-        quantize(w2_mx, w2_grouped, 0, N)
-        x_two_codes = w2_bytes.tile([P, N], U32, name="x_two_codes", offset=0, align_bytes=64)
-        x_idx_codes = w2_bytes.tile([P, N], U32, name="x_idx_codes", offset=4 * N, align_bytes=64)
         nc.vector.tensor_copy(x_two_codes[:], xw[:].indirect(two_sb[:]))
         nc.vector.tensor_copy(x_idx_codes[:], xw[:].indirect(offs_sb[:]))
-        x_idx_scales = keep.tile([P, N], U8, name="x_idx_scales", tag="xw", align_bytes=64)
-        nc.vector.tensor_copy(x_idx_scales[:], xs[:].indirect(offs_sb[:]))
-        x_two = (x_two_codes[:], x_two_scales[:])
-        x_idx = (x_idx_codes[:], x_idx_scales[:])
+        nc.vector.tensor_copy(x_two_scales[:], xs[:].indirect(two_sb[:]))
+
+        w2_grouped = keep.tile([P, PACK * N], BF16, name="w2_grouped", tag="w2_grouped", align_bytes=64)
+        dst, src = dealt_views(w2_grouped, w2_left)
+        nc.scalar.copy(dst[:, : P // 2], src)
+        dst, src = dealt_views(w2_grouped, w2_right)
+        nc.scalar.copy(dst[:, P // 2 : P // 2 + M_ON_SCALAR], src[:, :M_ON_SCALAR])
+        nc.vector.tensor_copy(dst[:, P // 2 + M_ON_SCALAR :], src[:, M_ON_SCALAR:])
+        w2_mx = mx_tiles("w2")
         b_banks = [psum.tile([P, N], F32, name="b_bank%d" % t, tag="bank%d" % t) for t in range(PACK)]
         for t in range(PACK):
-            product(b_banks[t], w2_mx, t, x_two)
+            quantize(w2_mx, w2_grouped, t * P, P)
+            product(b_banks[t], w2_mx, t, (x_two_codes[:], x_two_scales[:]))
+        x_idx_scales = keep.tile([P, N], U8, name="x_idx_scales", tag="w2_grouped", align_bytes=64)
+        nc.vector.tensor_copy(x_idx_scales[:], xs[:].indirect(offs_sb[:]))
+        x_idx = (x_idx_codes[:], x_idx_scales[:])
 
         w1_grouped = keep.tile([P, PACK * N], BF16, name="w1_grouped", tag="w1_grouped", align_bytes=64)
         dst, src = dealt_views(w1_grouped, w1_raw)
@@ -127,13 +133,23 @@ def tile_picked_keynorm_none_p_kernel(tc, x_words, x_scales, w1, w2, ga, gb, off
         for t in range(PACK):
             product(a_banks[t], w1_mx, t, x_idx)
 
+        last = PACK - 1
+        minus_gb = keep.tile([P, 1], F32, name="minus_gb")
+        size_gb = keep.tile([P, 1], F32, name="size_gb")
+        inv_size_gb = keep.tile([P, 1], F32, name="inv_size_gb", tag="w2_left")
+        nc.gpsimd.tensor_scalar_mul(minus_gb[:], gb_sb[:, last:], -1.0)
+        nc.gpsimd.tensor_scalar(size_gb[:], gb_sb[:, last:], SMALLEST_NORMAL, minus_gb[:], ALU.max, ALU.max)
+        nc.vector.reciprocal(inv_size_gb[:], size_gb[:])
+
         abs_b = keep.tile([P, PACK, N], F32, name="abs_b")
         b_rows = [w1_bytes.tile([P, N], F32, name="b_row%d" % t, offset=4 * N * t) for t in range(PACK)]
         for t in range(PACK):
-            nc.scalar.activation(abs_b[:, t, :], b_banks[t][:], ACT.Abs)
+            if t < last:
+                nc.scalar.activation(abs_b[:, t, :], b_banks[t][:], ACT.Abs)
             nc.vector.tensor_scalar_mul(b_rows[t][:], b_banks[t][:], gb_sb[:, t : t + 1])
+        nc.vector.scalar_tensor_tensor(abs_b[:, last, :], b_banks[last][:], minus_gb[:], b_rows[last][:], ALU.mult, ALU.max)
         log_b = keep.tile([P, PACK, N], F32, name="log_b", tag="log_b")
-        nc.scalar.activation(log_b[:], abs_b[:], ACT.Ln, bias=0.5)
+        nc.scalar.activation(log_b[:, :last, :], abs_b[:, :last, :], ACT.Ln, bias=0.5)
 
         b_picked = keep.tile([P, PACK, N], F32, name="b_picked", tag="w1_grouped", align_bytes=64)
         for t in range(PACK):
@@ -146,19 +162,22 @@ def tile_picked_keynorm_none_p_kernel(tc, x_words, x_scales, w1, w2, ga, gb, off
             nc.scalar.activation(abs_a[:, t, :], a_banks[t][:], ACT.Abs)
             nc.scalar.activation(log_a[t][:], abs_a[:, t, :], ACT.Ln, bias=0.5)
 
+        nc.scalar.activation(log_b[:, last, :], abs_b[:, last, :], ACT.Ln, bias=0.5, scale=inv_size_gb[:])
+
         inv_b = keep.tile([P, PACK, N], F32, name="inv_b", tag="abs_a")
         z2_grouped = keep.tile([P, PACK * N], BF16, name="z2_grouped", align_bytes=64)
         z2_mx = mx_tiles("z2")
-        for h in range(2):
-            cols = halves[h][0]
+        for first, end in ((0, HALF // 2), (HALF // 2, HALF), (HALF, N)):
+            cols = slice(first, end)
             nc.scalar.activation(inv_b[:, :, cols], log_b[:, :, cols], ACT.Exp, scale=-1.0)
             nc.vector.tensor_tensor(
-                z2_grouped[:, PACK * h * HALF : PACK * (h + 1) * HALF].rearrange("p (c i t) -> p c t i", i=4, t=PACK),
+                z2_grouped[:, PACK * first : PACK * end].rearrange("p (c i t) -> p c t i", i=4, t=PACK),
                 b_picked[:, :, cols].rearrange("p t (c i) -> p c t i", i=4),
                 inv_b[:, :, cols].rearrange("p t (c i) -> p c t i", i=4),
                 ALU.mult,
             )
-            quantize(z2_mx, z2_grouped, h * HALF, HALF)
+            if end % HALF == 0:
+                quantize(z2_mx, z2_grouped, end - HALF, HALF)
 
         inv_a = keep.tile([P, PACK, N], F32, name="inv_a", tag="log_b")
         z_planes = keep.tile([P, PACK, N], BF16, name="z_planes")
@@ -181,7 +200,6 @@ def tile_picked_keynorm_none_p_kernel(tc, x_words, x_scales, w1, w2, ga, gb, off
 
         z_mx = mx_tiles("z")
         out_rows = out.rearrange("(p t) v -> p t v", t=PACK)
-        last = PACK - 1
         first_banks = [psum.tile([P, HALF], F32, name="first_bank%d" % h, tag="bank%d" % (PACK * h)) for h in range(2)]
         s_banks = [None] + [psum.tile([P, N], F32, name="s_bank%d" % t, tag="bank%d" % t) for t in range(1, PACK)]
         rows = [keep.tile([P, N], F32, name="row%d" % t) for t in range(PACK)]
@@ -197,27 +215,27 @@ def tile_picked_keynorm_none_p_kernel(tc, x_words, x_scales, w1, w2, ga, gb, off
             quantize(z_mx, z_grouped, t * P, P)
             product(s_banks[t], z_mx, t, z2_mx)
         for h in range(2):
-            nc.vector.tensor_scalar_mul(rows[0][:, halves[h][0]], first_banks[h][:], 0.0625)
-        for t in range(1, last):
-            nc.vector.tensor_scalar_mul(rows[t][:], s_banks[t][:], 0.0625)
+            nc.scalar.activation(rows[0][:, halves[h][0]], first_banks[h][:], ACT.Copy, scale=0.0625)
 
         def gate_on_scalar(t):
             for cols, entries in halves:
                 nc.scalar.activation(gate[:, t, cols], rows[t][:].indirect(cq_sb[:, entries]), ACT.Sigmoid)
 
-        def finish(t, pieces):
-            for cols in pieces:
-                nc.vector.tensor_tensor(result[:, t, cols], rows[t][:, cols], gate[:, t, cols], ALU.mult)
-                nc.sync.dma_start(out_rows[:, t, cols], result[:, t, cols])
+        def finish(t, cols):
+            nc.vector.scalar_tensor_tensor(result[:, t, cols], s_banks[t][:, cols], 0.0625, gate[:, t, cols], ALU.mult, ALU.mult)
+            nc.sync.dma_start(out_rows[:, t, cols], result[:, t, cols])
 
+        nc.scalar.activation(rows[1][:], s_banks[1][:], ACT.Sigmoid, scale=0.0625)
         gate_on_scalar(0)
-        nc.scalar.activation(rows[last][:], s_banks[last][:], ACT.Sigmoid, scale=0.0625)
-        gate_on_scalar(1)
-        gate_on_scalar(2)
-        finish(0, [slice(0, N)])
+        nc.vector.tensor_scalar_mul(rows[2][:], s_banks[2][:], 0.0625)
         for cols, entries in halves:
-            nc.vector.tensor_copy(gate[:, last, cols], rows[last][:].indirect(cq_sb[:, entries]))
-        nc.vector.scalar_tensor_tensor(result[:, last, :], s_banks[last][:], 0.0625, gate[:, last, :], ALU.mult, ALU.mult)
-        nc.sync.dma_start(out_rows[:, last, :], result[:, last, :])
-        finish(1, [slice(0, N)])
-        finish(2, [cols for cols, entries in halves])
+            nc.vector.tensor_copy(gate[:, 1, cols], rows[1][:].indirect(cq_sb[:, entries]))
+        nc.vector.tensor_scalar_mul(rows[3][:], s_banks[3][:], 0.0625)
+        gate_on_scalar(2)
+        gate_on_scalar(3)
+        nc.gpsimd.tensor_tensor(result[:, 0, :], rows[0][:], gate[:, 0, :], ALU.mult)
+        nc.sync.dma_start(out_rows[:, 0, :], result[:, 0, :])
+        finish(1, slice(0, N))
+        finish(2, slice(0, N))
+        for cols, entries in halves:
+            finish(3, cols)

from contextlib import ExitStack

import concourse.mybir as mybir

F32 = mybir.dt.float32
BF16 = mybir.dt.bfloat16
I32 = mybir.dt.int32
U32 = mybir.dt.uint32
U16 = mybir.dt.uint16
U8 = mybir.dt.uint8
FP8X4 = mybir.dt.float8_e4m3fn_x4
ACT = mybir.ActivationFunctionType
ALU = mybir.AluOpType

P = 128
PACK = 4
T = 2048
N = 512
HALF = N // 2
LIST_COLS = N // 16
M_ON_SCALAR = 40

SMALLEST_NORMAL = 2.0**-126

FLOPS = 3 * 2 * 512 * 512 * 512


def tile_picked_keynorm_none_p_kernel(tc, x_words, x_scales, w1, w2, ga, gb, offs, two, n1, nq, cq, out):
    nc = tc.nc
    halves = [(slice(h * HALF, (h + 1) * HALF), slice(h * LIST_COLS // 2, (h + 1) * LIST_COLS // 2)) for h in range(2)]

    with ExitStack() as ctx:
        lists = ctx.enter_context(tc.tile_pool(name="lists", bufs=1))
        keep = ctx.enter_context(tc.tile_pool(name="keep", bufs=1))
        w1_bytes = ctx.enter_context(tc.tile_pool(name="w1_bytes", bufs=1))
        psum = ctx.enter_context(tc.psum_pool(name="psum", bufs=1))

        offs_sb = lists.tile([P, LIST_COLS], U16, name="offs_sb")
        two_sb = lists.tile([P, LIST_COLS], U16, name="two_sb")
        n1_sb = lists.tile([P, LIST_COLS], U16, name="n1_sb")
        nq_sb = lists.tile([P, LIST_COLS], U16, name="nq_sb")
        cq_sb = lists.tile([P, LIST_COLS], U16, name="cq_sb")

        xs = keep.tile([P, T], U8, name="xs", align_bytes=64)
        ga_sb = keep.tile([P, PACK], F32, name="ga_sb")
        gb_sb = keep.tile([P, PACK], F32, name="gb_sb")

        nc.vector.memset(xs[:].bitcast(I32), 0)
        one = keep.tile([P, 16], F32, name="one", tag="w2_left")
        nc.vector.memset(one[:], 1.0)
        warm_ln = w1_bytes.tile([P, 16], F32, name="warm_ln", offset=16 * N - 32)
        nc.scalar.activation(warm_ln[:], one[:], ACT.Ln)

        xw = keep.tile([P, T], U32, name="xw", align_bytes=64)
        w2_left = keep.tile([P, PACK, HALF], F32, name="w2_left", tag="w2_left")
        w2_right = w1_bytes.tile([P, PACK, HALF], F32, name="w2_right", offset=16 * N)
        w1_raw = w1_bytes.tile([P, PACK, N], F32, name="w1_raw", offset=0)

        nc.sync.dma_start(two_sb[:], two)
        nc.sync.dma_start(offs_sb[:], offs)
        nc.sync.dma_start(nq_sb[:], nq)
        nc.sync.dma_start(xw[:].bitcast(I32), x_words[0].rearrange("p n r -> p (n r)").bitcast(I32))
        nc.sync.dma_start(n1_sb[:], n1)
        nc.sync.dma_start(cq_sb[:], cq)
        for q in range(4):
            nc.sync.dma_start(xs[32 * q : 32 * q + 4, :].bitcast(I32), x_scales[0, 4 * q : 4 * q + 4, :].bitcast(I32))
        w2_rows = w2.rearrange("(p j) c -> p j c", j=PACK)
        nc.sync.dma_start(w2_left[:], w2_rows[:, :, :HALF])
        nc.sync.dma_start(w2_right[:], w2_rows[:, :, HALF:])
        nc.sync.dma_start(w1_raw[:], w1.rearrange("(p j) c -> p j c", j=PACK))
        nc.gpsimd.dma_start(gb_sb[:], gb.rearrange("(p t) o -> p (t o)", t=PACK))
        nc.gpsimd.dma_start(ga_sb[:], ga.rearrange("(p t) o -> p (t o)", t=PACK))

        def mx_tiles(name):
            codes = keep.tile([P, N], U32, name=name + "_codes", align_bytes=64)
            scales = keep.tile([P, N], U8, name=name + "_scales", align_bytes=64)
            return codes[:], scales[:]

        def quantize(dst, grouped, first, count):
            codes, scales = dst
            nc.vector.quantize_mx(
                out=codes[:, first : first + count].bitcast(FP8X4),
                scales=scales[:, first : first + count],
                in_=grouped[:, PACK * first : PACK * (first + count)],
            )

        def product(bank, stationary, t, moving):
            cols = slice(t * P, (t + 1) * P)
            nc.tensor.matmul_mx(
                out=bank[:],
                lhsT=stationary[0][:, cols].bitcast(FP8X4),
                lhsT_scale=stationary[1][:, cols],
                rhs=moving[0].bitcast(FP8X4),
                rhs_scale=moving[1],
                start=True,
                stop=True,
            )

        def dealt_views(grouped, planes):
            return (
                grouped[:].rearrange("p (t m j) -> p m j t", t=PACK, j=PACK),
                planes[:].rearrange("p j (m t) -> p m j t", t=PACK),
            )

        x_two_codes = keep.tile([P, N], U32, name="x_two_codes", align_bytes=64)
        x_idx_codes = keep.tile([P, N], U32, name="x_idx_codes", align_bytes=64)
        x_two_scales = keep.tile([P, N], U8, name="x_two_scales", align_bytes=64)
        nc.vector.tensor_copy(x_two_codes[:], xw[:].indirect(two_sb[:]))
        nc.vector.tensor_copy(x_idx_codes[:], xw[:].indirect(offs_sb[:]))
        nc.vector.tensor_copy(x_two_scales[:], xs[:].indirect(two_sb[:]))

        w2_grouped = keep.tile([P, PACK * N], BF16, name="w2_grouped", tag="w2_grouped", align_bytes=64)
        dst, src = dealt_views(w2_grouped, w2_left)
        nc.scalar.copy(dst[:, : P // 2], src)
        dst, src = dealt_views(w2_grouped, w2_right)
        nc.scalar.copy(dst[:, P // 2 : P // 2 + M_ON_SCALAR], src[:, :M_ON_SCALAR])
        nc.vector.tensor_copy(dst[:, P // 2 + M_ON_SCALAR :], src[:, M_ON_SCALAR:])
        w2_mx = mx_tiles("w2")
        b_banks = [psum.tile([P, N], F32, name="b_bank%d" % t, tag="bank%d" % t) for t in range(PACK)]
        for t in range(PACK):
            quantize(w2_mx, w2_grouped, t * P, P)
            product(b_banks[t], w2_mx, t, (x_two_codes[:], x_two_scales[:]))
        x_idx_scales = keep.tile([P, N], U8, name="x_idx_scales", tag="w2_grouped", align_bytes=64)
        nc.vector.tensor_copy(x_idx_scales[:], xs[:].indirect(offs_sb[:]))
        x_idx = (x_idx_codes[:], x_idx_scales[:])

        w1_grouped = keep.tile([P, PACK * N], BF16, name="w1_grouped", tag="w1_grouped", align_bytes=64)
        dst, src = dealt_views(w1_grouped, w1_raw)
        nc.vector.tensor_copy(dst, src)
        w1_mx = mx_tiles("w1")
        a_banks = [psum.tile([P, N], F32, name="a_bank%d" % t, tag="bank%d" % (PACK + t)) for t in range(PACK)]
        quantize(w1_mx, w1_grouped, 0, N)
        for t in range(PACK):
            product(a_banks[t], w1_mx, t, x_idx)

        last = PACK - 1
        minus_gb = keep.tile([P, 1], F32, name="minus_gb")
        size_gb = keep.tile([P, 1], F32, name="size_gb")
        inv_size_gb = keep.tile([P, 1], F32, name="inv_size_gb", tag="w2_left")
        nc.gpsimd.tensor_scalar_mul(minus_gb[:], gb_sb[:, last:], -1.0)
        nc.gpsimd.tensor_scalar(size_gb[:], gb_sb[:, last:], SMALLEST_NORMAL, minus_gb[:], ALU.max, ALU.max)
        nc.vector.reciprocal(inv_size_gb[:], size_gb[:])

        abs_b = keep.tile([P, PACK, N], F32, name="abs_b")
        b_rows = [w1_bytes.tile([P, N], F32, name="b_row%d" % t, offset=4 * N * t) for t in range(PACK)]
        for t in range(PACK):
            if t < last:
                nc.scalar.activation(abs_b[:, t, :], b_banks[t][:], ACT.Abs)
            nc.vector.tensor_scalar_mul(b_rows[t][:], b_banks[t][:], gb_sb[:, t : t + 1])
        nc.vector.scalar_tensor_tensor(abs_b[:, last, :], b_banks[last][:], minus_gb[:], b_rows[last][:], ALU.mult, ALU.max)
        log_b = keep.tile([P, PACK, N], F32, name="log_b", tag="log_b")
        nc.scalar.activation(log_b[:, :last, :], abs_b[:, :last, :], ACT.Ln, bias=0.5)

        b_picked = keep.tile([P, PACK, N], F32, name="b_picked", tag="w1_grouped", align_bytes=64)
        for t in range(PACK):
            for cols, entries in halves:
                nc.vector.tensor_copy(b_picked[:, t, cols], b_rows[t][:].indirect(nq_sb[:, entries]))

        abs_a = keep.tile([P, PACK, N], F32, name="abs_a", tag="abs_a")
        log_a = [keep.tile([P, N], F32, name="log_a%d" % t) for t in range(PACK)]
        for t in range(PACK):
            nc.scalar.activation(abs_a[:, t, :], a_banks[t][:], ACT.Abs)
            nc.scalar.activation(log_a[t][:], abs_a[:, t, :], ACT.Ln, bias=0.5)

        nc.scalar.activation(log_b[:, last, :], abs_b[:, last, :], ACT.Ln, bias=0.5, scale=inv_size_gb[:])

        inv_b = keep.tile([P, PACK, N], F32, name="inv_b", tag="abs_a")
        z2_grouped = keep.tile([P, PACK * N], BF16, name="z2_grouped", align_bytes=64)
        z2_mx = mx_tiles("z2")
        for first, end in ((0, HALF // 2), (HALF // 2, HALF), (HALF, N)):
            cols = slice(first, end)
            nc.scalar.activation(inv_b[:, :, cols], log_b[:, :, cols], ACT.Exp, scale=-1.0)
            nc.vector.tensor_tensor(
                z2_grouped[:, PACK * first : PACK * end].rearrange("p (c i t) -> p c t i", i=4, t=PACK),
                b_picked[:, :, cols].rearrange("p t (c i) -> p c t i", i=4),
                inv_b[:, :, cols].rearrange("p t (c i) -> p c t i", i=4),
                ALU.mult,
            )
            if end % HALF == 0:
                quantize(z2_mx, z2_grouped, end - HALF, HALF)

        inv_a = keep.tile([P, PACK, N], F32, name="inv_a", tag="log_b")
        z_planes = keep.tile([P, PACK, N], BF16, name="z_planes")
        z_grouped = keep.tile([P, PACK * N], BF16, name="z_grouped", align_bytes=64)
        dst, src = dealt_views(z_grouped, z_planes)
        for h in range(2):
            cols, entries = halves[h]
            for t in range(PACK):
                nc.scalar.activation(inv_a[:, t, cols], log_a[t][:].indirect(n1_sb[:, entries]), ACT.Exp, scale=-1.0)
                nc.vector.scalar_tensor_tensor(
                    z_planes[:, t, cols], a_banks[t][:, cols], ga_sb[:, t : t + 1], inv_a[:, t, cols], ALU.mult, ALU.mult
                )
            ms = slice(h * P // 2, (h + 1) * P // 2)
            if h == 0:
                nc.vector.tensor_copy(dst[:, ms], src[:, ms])
            else:
                nc.vector.tensor_copy(dst[:, ms, :, :1], src[:, ms, :, :1])
        warm_sigmoid = keep.tile([P, 1], F32, name="warm_sigmoid")
        nc.scalar.activation(warm_sigmoid[:], inv_a[:, PACK - 1, N - 1 : N], ACT.Sigmoid)

        z_mx = mx_tiles("z")
        out_rows = out.rearrange("(p t) v -> p t v", t=PACK)
        first_banks = [psum.tile([P, HALF], F32, name="first_bank%d" % h, tag="bank%d" % (PACK * h)) for h in range(2)]
        s_banks = [None] + [psum.tile([P, N], F32, name="s_bank%d" % t, tag="bank%d" % t) for t in range(1, PACK)]
        rows = [keep.tile([P, N], F32, name="row%d" % t) for t in range(PACK)]
        gate = keep.tile([P, PACK, N], F32, name="gate")
        result = keep.tile([P, PACK, N], F32, name="result")

        quantize(z_mx, z_grouped, 0, P)
        for h in range(2):
            cols = halves[h][0]
            product(first_banks[h], z_mx, 0, (z2_mx[0][:, cols], z2_mx[1][:, cols]))
        nc.vector.tensor_copy(dst[:, P // 2 :, :, 1:], src[:, P // 2 :, :, 1:])
        for t in range(1, PACK):
            quantize(z_mx, z_grouped, t * P, P)
            product(s_banks[t], z_mx, t, z2_mx)
        for h in range(2):
            nc.scalar.activation(rows[0][:, halves[h][0]], first_banks[h][:], ACT.Copy, scale=0.0625)

        def gate_on_scalar(t):
            for cols, entries in halves:
                nc.scalar.activation(gate[:, t, cols], rows[t][:].indirect(cq_sb[:, entries]), ACT.Sigmoid)

        def finish(t, cols):
            nc.vector.scalar_tensor_tensor(result[:, t, cols], s_banks[t][:, cols], 0.0625, gate[:, t, cols], ALU.mult, ALU.mult)
            nc.sync.dma_start(out_rows[:, t, cols], result[:, t, cols])

        nc.scalar.activation(rows[1][:], s_banks[1][:], ACT.Sigmoid, scale=0.0625)
        gate_on_scalar(0)
        nc.vector.tensor_scalar_mul(rows[2][:], s_banks[2][:], 0.0625)
        for cols, entries in halves:
            nc.vector.tensor_copy(gate[:, 1, cols], rows[1][:].indirect(cq_sb[:, entries]))
        nc.vector.tensor_scalar_mul(rows[3][:], s_banks[3][:], 0.0625)
        gate_on_scalar(2)
        gate_on_scalar(3)
        nc.gpsimd.tensor_tensor(result[:, 0, :], rows[0][:], gate[:, 0, :], ALU.mult)
        nc.sync.dma_start(out_rows[:, 0, :], result[:, 0, :])
        finish(1, slice(0, N))
        finish(2, slice(0, N))
        for cols, entries in halves:
            finish(3, cols)
